import numpy as np
import ml_dtypes


def mxq(x, axis, fmt="e4m3"):
    dtype, down = {"e4m3": (ml_dtypes.float8_e4m3fn, 7), "e5m2": (ml_dtypes.float8_e5m2, 14)}[fmt]
    v = np.moveaxis(np.asarray(x, np.float32).astype(ml_dtypes.bfloat16).astype(np.float64), axis, -1)
    blocks = v.reshape(v.shape[:-1] + (-1, 32))
    amax = np.abs(blocks).max(-1, keepdims=True)
    byte = np.maximum(np.where(amax > 0, np.frexp(amax)[1] - 1 + 127, 0) - down, 1)
    scale = np.exp2(byte - 127.0)
    codes = (blocks / scale).astype(np.float32).astype(dtype).astype(np.float64)
    return np.moveaxis((codes * scale).reshape(v.shape), -1, axis)


WIDE = False


def mx_kscale(k):
    if not WIDE:
        return np.ones(k)
    levels = np.array([10, -10, 5, -5, 0])
    if k % 512:
        return np.exp2(np.random.permutation(np.resize(levels, k // 32))).repeat(32)
    a = np.empty((k // 512, 16))
    for p in range(k // 512):
        a[p, :8] = np.random.permutation(np.resize(levels, 8))
        for g in range(8):
            far = levels[np.abs(levels - a[p, g]) >= 10]
            a[p, g + 8] = far[np.random.randint(len(far))]
    return np.exp2(a.ravel()).repeat(32)


def f64(x):
    return np.asarray(x).astype(np.float64)


def striped(idx):
    return np.tile(idx.reshape(-1, 16).T, (8, 1)).astype(np.uint16)


def unstriped(offs):
    return offs[:16].T.reshape(-1).astype(np.int64)


E2M1 = np.array([0.0, 0.5, 1.0, 1.5, 2.0, 3.0, 4.0, 6.0, -0.0, -0.5, -1.0, -1.5, -2.0, -3.0, -4.0, -6.0])


def pack_weight(w, fmt):
    k, n = w.shape
    w = f64(np.asarray(w, np.float32).astype(ml_dtypes.bfloat16)).reshape(k // 32, 32, n)
    amax = np.abs(w).max(1)
    if fmt == "e4m3":
        byte = np.frexp(amax)[1] - 1 + 127 - 7
    else:
        mant, ex = np.frexp(amax / 6.0)
        byte = np.where(mant > 0.5, ex, ex - 1) + 127
    byte = np.clip(np.where(amax > 0, byte, 1), 1, 254)
    scaled = (w * np.exp2(127.0 - byte)[:, None, :]).reshape(k, n).astype(np.float32)
    by_word = np.ascontiguousarray(scaled.reshape(k // 512, 128, 4, n).transpose(0, 1, 3, 2))
    if fmt == "e4m3":
        words = by_word.astype(ml_dtypes.float8_e4m3fn).view(np.uint8)
    else:
        c = by_word.astype(ml_dtypes.float4_e2m1fn).view(np.uint8) & 0xF
        words = (c[..., 0::2] | (c[..., 1::2] << 4)).reshape(k // 512, 128, 2 * n)
    return np.ascontiguousarray(words), np.ascontiguousarray(byte.astype(np.uint8).reshape(k // 512, 16, n))


def unpack_weight(words, scales, fmt):
    g, _, n = scales.shape
    words = np.ascontiguousarray(words).reshape(g, 128, n, -1)
    if fmt == "e4m3":
        vals = words.view(ml_dtypes.float8_e4m3fn).astype(np.float64)
    else:
        nib = np.empty((g, 128, n, 4), np.uint8)
        nib[..., 0::2] = words & 0xF
        nib[..., 1::2] = words >> 4
        vals = E2M1[nib]
    vals = vals * np.repeat(np.exp2(scales.astype(np.float64) - 127.0), 8, axis=1)[..., None]
    return vals.transpose(0, 1, 3, 2).reshape(g * 512, n)


def gelu(v):
    return 0.5 * v * (1.0 + np.tanh(np.sqrt(2.0 / np.pi) * (v + 0.044715 * v**3)))


K, H, T, S, T2, P = 1536, 1024, 2048, 512, 1024, 512

def setup_inputs():
    n = np.random.standard_normal
    s = mx_kscale(K)[:, None]
    u = mx_kscale(H)[:, None]
    d = {}
    d["tab_words"], d["tab_scales"] = pack_weight(n((K, T)) * s, "e4m3")
    d["offs"] = striped(np.random.permutation(T)[:S])
    d["offs2"] = striped(np.random.permutation(T2)[:S])
    d["offs3"] = striped(np.random.permutation(T2)[:P])
    d["w1"] = (n((K, H)) / K**0.5 / s).astype(np.float32)
    d["w4_words"], d["w4_scales"] = pack_weight(n((K, H)) / K**0.5 / s, "e2m1")
    d["cap"] = n((H, S)).astype(np.float32)
    d["gain"] = (np.exp(0.3 * n(H)) * u[:, 0]).astype(np.float32)
    d["page0"] = (n((H, T2)) * u).astype(np.float32)
    d["wgs"] = np.exp(0.3 * n((128, S))).astype(np.float32)
    d["lows"] = (0.4 * n(H) * u[:, 0]).astype(np.float32)
    d["vec"] = (1.3 * n(H) / H**0.5 / u[:, 0]**2).astype(np.float32)
    d["q"] = (1.1 * n((H, P)) / H**0.5 / u).astype(np.float32)
    d["slot"] = (0.5 * n(T2)).astype(np.float32)
    return d

def reference(tab_words, tab_scales, offs, offs2, offs3, w1, w4_words, w4_scales, cap, gain, page0, wgs, lows, vec, q, slot):
    v = unpack_weight(tab_words, tab_scales, "e4m3")[:, unstriped(offs)]
    w4 = unpack_weight(w4_words, w4_scales, "e2m1")
    a = mxq(f64(w1), 0, "e4m3").T @ v
    b = w4.T @ v
    h = f64(gain)[:, None] * np.tanh(b - np.minimum(a, f64(cap)))
    page = f64(page0).copy()
    page[:, unstriped(offs2)] = np.tile(f64(wgs), (H // 128, 1)) * h
    x = np.maximum(page[:, unstriped(offs3)], f64(lows)[:, None]) * f64(vec)[:, None]
    pq = mxq(page, 0, "e4m3")
    e = pq.T @ mxq(x, 0, "e4m3")
    f = pq.T @ mxq(f64(q), 0, "e4m3")
    return e * f + f64(slot)[:, None]

@@ -1,0 +1,479 @@
+from contextlib import ExitStack
+
+import concourse.mybir as mybir
+
+K, H, T, S, T2, NP = 1536, 1024, 2048, 512, 1024, 512
+FLOPS = 2 * (2 * K * H * S + 2 * H * T2 * NP)
+
+F32 = mybir.dt.float32
+BF16 = mybir.dt.bfloat16
+I32 = mybir.dt.int32
+U32 = mybir.dt.uint32
+U16 = mybir.dt.uint16
+U8 = mybir.dt.uint8
+FP8X4 = mybir.dt.float8_e4m3fn_x4
+FP4X4 = mybir.dt.float4_e2m1fn_x4
+ALU = mybir.AluOpType
+ACT = mybir.ActivationFunctionType
+
+P = 128
+PACK = 4
+KP = P * PACK
+KA = K // KP
+HB = H // KP
+SLICES = HB * PACK
+MT = T2 // P
+PIECE = 256
+RUN = 4
+
+
+def tile_list_darts_slot_scores_kernel(
+    tc, tab_words, tab_scales, offs, offs2, offs3, w1, w4_words, w4_scales, cap, gain, page0, wgs, lows, vec, q, slot, out
+):
+    nc = tc.nc
+    with ExitStack() as ctx:
+        keep = ctx.enter_context(tc.tile_pool(name="keep", bufs=1))
+        ring = ctx.enter_context(tc.tile_pool(name="ring", bufs=1))
+        psum = ctx.enter_context(tc.psum_pool(name="psum", bufs=1))
+
+        def kept(shape, dtype, name, tag=None):
+            return keep.tile(shape, dtype, name=name, tag=tag or name, align_bytes=64)
+
+        def ringed(shape, dtype, name, tag, bufs):
+            return ring.tile(shape, dtype, name=name, tag=tag, bufs=bufs, align_bytes=64)
+
+        def raw_tile(shape, name):
+            return ringed(shape, F32, name, "raw", 4)
+
+        def bank(n, name):
+            return psum.tile([P, 512], F32, name=name, tag="bank%d" % n)
+
+        def quantize(codes, scales, values):
+            nc.vector.quantize_mx(out=codes.bitcast(FP8X4), scales=scales, in_=values)
+
+        idx = keep.tile([P, S // 16], U16, name="idx")
+        idx2 = keep.tile([P, S // 16], U16, name="idx2")
+        idx3 = keep.tile([P, NP // 16], U16, name="idx3")
+
+        tab_s = kept([P, KA, T], U8, "tab_s")
+        w4_s_raw = kept([P, KA, H], U8, "w4_s_raw")
+        nc.vector.memset(tab_s[:].rearrange("p a n -> p (a n)").bitcast(I32), 0)
+        nc.vector.memset(w4_s_raw[:].rearrange("p a n -> p (a n)").bitcast(I32), 0)
+
+        vectors = kept([P, HB, P], F32, "vectors")
+        nc.vector.memset(vectors[:], 0.0)
+
+        warm = kept([P, 2], F32, "warm")
+        nc.vector.memset(warm[:, 0:1], 0.0)
+        warm_out = kept([P, 1], F32, "warm_out")
+        nc.scalar.activation(warm_out[:], warm[:, 0:1], ACT.Tanh)
+
+        tab_w = [kept([P, T], I32, "tab_w%d" % a) for a in range(KA)]
+
+        def load_tab(a):
+            nc.sync.dma_start(tab_w[a][:], tab_words[a].rearrange("p n i -> p (n i)").bitcast(I32))
+
+        w1_rows = w1.rearrange("(a p j) c -> a p j c", p=P, j=PACK)
+
+        def load_w1(a, c0, width):
+            raw = raw_tile([P, PACK, width], "w1_raw%d_%d" % (a, c0))
+            nc.sync.dma_start(raw[:], w1_rows[a][:, :, c0 : c0 + width])
+            return raw
+
+        cap_rows = cap.rearrange("(b u t e) s -> b t u e s", b=HB, t=PACK, e=RUN)
+        page_rows = page0.rearrange("(b u t e) m -> b t u e m", b=HB, t=PACK, e=RUN)
+        caps, pages = {}, {}
+
+        def load_cap(i):
+            caps[i] = ringed([P, S], F32, "cap%d" % i, "cap", 4)
+            nc.sync.dma_start(caps[i][:], cap_rows[i // PACK][i % PACK])
+
+        def load_page(i):
+            pages[i] = kept([P, T2], F32, "page%d" % i)
+            nc.sync.dma_start(pages[i][:], page_rows[i // PACK][i % PACK])
+
+        nc.sync.dma_start(idx[:], offs)
+        load_tab(0)
+        for quad in range(4):
+            rows = tab_scales[:, 4 * quad : 4 * quad + 4, :].rearrange("a r n -> r a n")
+            nc.sync.dma_start(tab_s[32 * quad : 32 * quad + 4].bitcast(I32), rows.bitcast(I32))
+        for quad in range(4):
+            rows = w4_scales[:, 4 * quad : 4 * quad + 4, :].rearrange("a r n -> r a n")
+            nc.sync.dma_start(w4_s_raw[32 * quad : 32 * quad + 4].bitcast(I32), rows.bitcast(I32))
+        for row, vector in enumerate((gain, lows, vec)):
+            nc.sync.dma_start(vectors[row:P:32], vector.rearrange("(b g c) -> g b c", b=HB, g=4))
+        w4_raw = kept([P, KA, H // 2], I32, "w4_raw")
+        nc.sync.dma_start(w4_raw[:], w4_words.rearrange("a p n -> p a n").bitcast(I32))
+        w1_raw = {}
+        w1_raw[0, 0] = load_w1(0, 0, KP)
+        load_tab(1)
+        w1_raw[1, 0] = load_w1(1, 0, KP)
+        load_tab(2)
+        w1_last = [load_w1(2, half * (KP // 2), KP // 2) for half in range(2)]
+        load_cap(0)
+        wgs_rows = wgs.rearrange("(u t e) s -> t u e s", t=PACK, e=RUN)
+        wgs_t = [kept([P, S], F32, "wgs_t%d" % t) for t in range(PACK)]
+
+        def load_wgs(t):
+            for quad in range(4):
+                nc.sync.dma_start(wgs_t[t][32 * quad : 32 * quad + 32], wgs_rows[t])
+
+        load_wgs(0)
+        nc.sync.dma_start(idx2[:], offs2)
+        load_cap(1)
+        load_page(0)
+        nc.sync.dma_start(idx3[:], offs3)
+        load_page(1)
+        load_wgs(1)
+        load_cap(2)
+        load_wgs(2)
+        load_cap(3)
+        load_wgs(3)
+
+        v_w = [kept([P, S], U32, "v_w%d" % a) for a in range(KA)]
+        v_s = [kept([P, S], U8, "v_s%d" % a) for a in range(KA)]
+
+        def gather_words(a):
+            nc.vector.tensor_copy(v_w[a][:], tab_w[a][:].bitcast(U32).indirect(idx[:]))
+
+        gather_words(0)
+        for a in range(KA):
+            nc.vector.tensor_copy(v_s[a][:], tab_s[:, a, :].indirect(idx[:]))
+
+        w4_s = kept([P, KA * HB, PACK, P], U8, "w4_s")
+        nc.vector.tensor_copy(
+            w4_s[:].bitcast(I32).rearrange("p g t u -> p g u t"),
+            w4_s_raw[:].bitcast(I32).rearrange("p a (b u t) -> p (a b) u t", b=HB, t=PACK),
+        )
+        w4_w = kept([P, KA * HB, PACK, P // 2], I32, "w4_w")
+        nc.vector.tensor_copy(
+            w4_w[:].rearrange("p g t (u e) -> p g u t e", e=2),
+            w4_raw[:].rearrange("p a (b u t e) -> p (a b) u t e", b=HB, t=PACK, e=2),
+        )
+
+        vectors_dealt = kept([P, SLICES * 32], F32, "vectors_dealt")
+        nc.vector.tensor_copy(
+            vectors_dealt[:].rearrange("p (b t u e) -> p b u t e", b=HB, t=PACK, e=RUN),
+            vectors[:].rearrange("p b (u t e) -> p b u t e", t=PACK, e=RUN),
+        )
+        per_row = kept([P, SLICES * 32], F32, "per_row")
+        nc.vector.transpose(per_row[:], vectors_dealt[:])
+
+        w1_w, w1_s = {}, {}
+        shared = [kept([P, KP * PACK // 2], F32, "shared%d" % b) for b in range(HB)]
+
+        def rounded_tile(name):
+            return ringed([P, KP * PACK], BF16, name, "rounded", 2)
+
+        def round_w1(a, b):
+            if (a, b) == (KA - 1, HB - 1):
+                rounded = shared[0][:].bitcast(BF16)
+            else:
+                rounded = rounded_tile("w1_bf%d_%d" % (a, b))[:]
+            nc.scalar.copy(
+                rounded.rearrange("p (t u e j) -> p u t j e", t=PACK, e=RUN, j=PACK),
+                w1_raw[a, b][:].rearrange("p j (u t e) -> p u t j e", t=PACK, e=RUN),
+            )
+            return rounded
+
+        def quantize_w1(a, b, rounded):
+            w1_w[a, b] = kept([P, KP], U32, "w1_w%d_%d" % (a, b))
+            w1_s[a, b] = kept([P, KP], U8, "w1_s%d_%d" % (a, b))
+            quantize(w1_w[a, b][:], w1_s[a, b][:], rounded)
+
+        rounded = round_w1(0, 0)
+        gather_words(1)
+        quantize_w1(0, 0, rounded)
+        rounded = round_w1(1, 0)
+        gather_words(2)
+        quantize_w1(1, 0, rounded)
+        rounded = rounded_tile("w1_bf2_0")[:]
+        halves = rounded.rearrange("p (t h u e j) -> p h u t j e", t=PACK, h=2, e=RUN, j=PACK)
+        nc.scalar.copy(halves[:, 0], w1_last[0][:].rearrange("p j (u t e) -> p u t j e", t=PACK, e=RUN))
+        nc.vector.tensor_copy(halves[:, 1], w1_last[1][:].rearrange("p j (u t e) -> p u t j e", t=PACK, e=RUN))
+        quantize_w1(2, 0, rounded)
+
+        sums, lesser, tanhs, factors, picked = {}, {}, {}, {}, {}
+
+        def first_products(i):
+            b, t = divmod(i, PACK)
+            a_sum = bank(2 * i % 8, "a_sum%d" % i)
+            b_sum = bank((2 * i + 1) % 8, "b_sum%d" % i)
+            cols = slice(t * P, (t + 1) * P)
+            for a in range(KA):
+                nc.tensor.matmul_mx(
+                    out=b_sum[:],
+                    lhsT=w4_w[:, a * HB + b, t, :].bitcast(FP4X4),
+                    lhsT_scale=w4_s[:, a * HB + b, t, :],
+                    rhs=v_w[a][:].bitcast(FP8X4),
+                    rhs_scale=v_s[a][:],
+                    start=(a == 0),
+                    stop=(a == KA - 1),
+                )
+                nc.tensor.matmul_mx(
+                    out=a_sum[:],
+                    lhsT=w1_w[a, b][:, cols].bitcast(FP8X4),
+                    lhsT_scale=w1_s[a, b][:, cols],
+                    rhs=v_w[a][:].bitcast(FP8X4),
+                    rhs_scale=v_s[a][:],
+                    start=(a == 0),
+                    stop=(a == KA - 1),
+                )
+            sums[i] = (a_sum, b_sum)
+
+        def take_min(i):
+            lesser[i] = ringed([P, S], F32, "lesser%d" % i, "lesser", 2)
+            nc.vector.tensor_tensor(lesser[i][:], sums[i][0][:], caps[i][:], ALU.min)
+
+        diffs = {}
+
+        def subtract(i):
+            diffs[i] = ringed([P, S], F32, "diff%d" % i, "diff", 2)
+            nc.vector.tensor_tensor(diffs[i][:], sums[i][1][:], lesser[i][:], ALU.subtract)
+
+        def make_factor(i, home=None):
+            factors[i] = ringed([P, S], F32, "factor%d" % i, "factor", 3)[:] if home is None else home[:, 0:S]
+            nc.scalar.activation(factors[i], wgs_t[i % PACK][:], ACT.Copy, scale=per_row[:, 32 * i : 32 * i + 1])
+
+        def make_tanh(i, home=None):
+            tanhs[i] = ringed([P, S], F32, "tanh%d" % i, "tanh", 3)[:] if home is None else home[:, 0:S]
+            nc.scalar.activation(tanhs[i], diffs[i][:], ACT.Tanh)
+
+        def scatter(i):
+            nc.vector.tensor_tensor(pages[i][:].indirect(idx2[:]), tanhs[i], factors[i], ALU.mult)
+
+        def gather_page(i, home=None):
+            picked[i] = ringed([P, NP], F32, "picked%d" % i, "picked", 2)[:] if home is None else home[:, 0:NP]
+            nc.vector.tensor_copy(picked[i], pages[i][:].indirect(idx3[:]))
+
+        def make_x(i, target):
+            nc.vector.tensor_scalar(
+                target, picked[i], per_row[:, 32 * i + 1 : 32 * i + 2], per_row[:, 32 * i + 2 : 32 * i + 3], ALU.max, ALU.mult
+            )
+
+        def interleave(target, rows, t0):
+            n = rows.shape[1]
+            nc.scalar.copy(
+                target[:, :, t0 : t0 + n].rearrange("p (c i) t -> p c t i", i=4),
+                rows.rearrange("p t (c i) -> p c t i", i=4),
+            )
+
+        x_rows = [kept([P, PACK, NP], BF16, "x_rows0"), kept([P, 2, NP], BF16, "x_rows1")]
+        x_bf = [shared[b][:].bitcast(BF16).rearrange("p (n t) -> p n t", t=PACK) for b in range(HB)]
+        x_w = [kept([P, NP], U32, "x_w%d" % b) for b in range(HB)]
+        x_s = [kept([P, NP], U8, "x_s%d" % b) for b in range(HB)]
+        q_w = [kept([P, NP], U32, "q_w%d" % b) for b in range(HB)]
+        q_s = [kept([P, NP], U8, "q_s%d" % b) for b in range(HB)]
+        pieces = T2 // PIECE
+        page_home = [[kept([P, PIECE * PACK // 2], F32, "page_bf%d_%d" % (b, n)) for n in range(pieces)] for b in range(HB)]
+        page_bf = [[home[:].bitcast(BF16).rearrange("p (n t) -> p n t", t=PACK) for home in homes] for homes in page_home]
+        page_w = [[kept([P, PIECE], U32, "page_w%d_%d" % (b, n)) for n in range(pieces)] for b in range(HB)]
+        page_s = [[kept([P, PIECE], U8, "page_s%d_%d" % (b, n)) for n in range(pieces)] for b in range(HB)]
+
+        def quantize_x(b):
+            quantize(x_w[b][:], x_s[b][:], shared[b][:].bitcast(BF16))
+
+        def quantize_page(b, n):
+            quantize(page_w[b][n][:], page_s[b][n][:], page_home[b][n][:].bitcast(BF16))
+
+        def round_q(b, raw):
+            if b == 0:
+                rounded_q = rounded_tile("q_bf0")[:]
+            else:
+                rounded_q = shared[1][:].bitcast(BF16)
+            interleave(rounded_q.rearrange("p (n t) -> p n t", t=PACK), raw[:], 0)
+            return rounded_q
+
+        def round_page_slice(i, n):
+            b, t = divmod(i, PACK)
+            nc.scalar.copy(page_bf[b][n][:, :, t], pages[i][:, n * PIECE : (n + 1) * PIECE])
+
+        q_rows = q.rearrange("(b u t e) s -> b t u e s", b=HB, t=PACK, e=RUN)
+        e_sum, f_sum = {}, {}
+
+        def second_pass(acc, c, b, moving_w, moving_s):
+            n, cols = c // 2, slice(c % 2 * P, (c % 2 + 1) * P)
+            nc.tensor.matmul_mx(
+                out=acc[:],
+                lhsT=page_w[b][n][:, cols].bitcast(FP8X4),
+                lhsT_scale=page_s[b][n][:, cols],
+                rhs=moving_w[b][:].bitcast(FP8X4),
+                rhs_scale=moving_s[b][:],
+                start=(b == 0),
+                stop=(b == HB - 1),
+            )
+
+        def open_sums(c):
+            f_sum[c] = bank(2 * c % 8, "f_sum%d" % c)
+            e_sum[c] = bank((2 * c + 1) % 8, "e_sum%d" % c)
+            second_pass(f_sum[c], c, 0, q_w, q_s)
+            second_pass(e_sum[c], c, 0, x_w, x_s)
+
+        def min_of(i):
+            if i >= PACK:
+                first_products(i)
+            take_min(i)
+
+        def load_q(b):
+            raw = raw_tile([P, PACK, NP], "q_raw%d" % b)
+            for t in range(PACK):
+                nc.sync.dma_start(raw[:, t, :], q_rows[b][t])
+            return raw
+
+        for i in range(PACK):
+            first_products(i)
+        take_min(0)
+        subtract(0)
+        make_factor(0)
+        make_tanh(0)
+        take_min(1)
+        subtract(1)
+        make_factor(1)
+        make_tanh(1)
+
+        w1_raw[0, 1] = load_w1(0, KP, KP)
+        w1_raw[1, 1] = load_w1(1, KP, KP)
+        load_page(2)
+        w1_raw[2, 1] = load_w1(2, KP, KP)
+
+        scatter(0)
+        min_of(2)
+        gather_page(0)
+        subtract(2)
+        make_x(0, x_rows[0][:, 0, :])
+        make_factor(2)
+        make_tanh(2)
+        load_cap(4)
+        load_page(3)
+        q_raw = [load_q(0)]
+
+        rounded = round_w1(0, 1)
+        scatter(1)
+        quantize_w1(0, 1, rounded)
+        min_of(3)
+        gather_page(1)
+        subtract(3)
+        make_x(1, x_rows[0][:, 1, :])
+        make_tanh(3)
+        load_cap(5)
+        load_page(4)
+        q_raw.append(load_q(1))
+
+        rounded = round_w1(1, 1)
+        rounded_last = round_w1(2, 1)
+        scatter(2)
+        quantize_w1(1, 1, rounded)
+        quantize_w1(2, 1, rounded_last)
+        make_factor(3, shared[0])
+        gather_page(2)
+        make_x(2, x_rows[0][:, 2, :])
+        load_cap(6)
+        load_page(5)
+        load_cap(7)
+        load_page(6)
+        load_page(7)
+        slot_t = kept([P, MT], F32, "slot_t")
+        with nc.allow_non_contiguous_dma(reason="one value of slot for each output row"):
+            nc.sync.dma_start(slot_t[:], slot.rearrange("(c p) -> p c", p=P))
+
+        q_bf = [round_q(0, q_raw[0])]
+        scatter(3)
+        min_of(4)
+        gather_page(3)
+        subtract(4)
+        make_x(3, x_rows[0][:, 3, :])
+        make_factor(4)
+        make_tanh(4)
+        min_of(5)
+        quantize(q_w[0][:], q_s[0][:], q_bf[0])
+        subtract(5)
+        make_tanh(5)
+        staged = [raw_tile([P, PACK, T2 // 2], "staged%d" % half) for half in range(2)]
+        for half in range(2):
+            for t in range(PACK):
+                nc.sync.dma_start(staged[half][:, t, :], pages[t][:, half * (T2 // 2) : (half + 1) * (T2 // 2)])
+        q_bf.append(round_q(1, q_raw[1]))
+
+        scatter(4)
+        quantize(q_w[1][:], q_s[1][:], q_bf[1])
+        make_factor(5, shared[1])
+        min_of(6)
+        gather_page(4)
+        subtract(6)
+        make_x(4, x_rows[1][:, 0, :])
+        make_tanh(6)
+        interleave(x_bf[0], x_rows[0][:], 0)
+        for n in range(pieces):
+            interleave(page_bf[0][n], staged[n // 2][:, :, n % 2 * PIECE : (n % 2 + 1) * PIECE], 0)
+        staged_pair = raw_tile([P, 2, T2], "staged_pair")
+        nc.sync.dma_start(staged_pair[:, 0, :], pages[4][:])
+
+        scatter(5)
+        quantize_page(0, 0)
+        quantize_page(0, 1)
+        make_factor(6, page_home[0][1])
+        min_of(7)
+        gather_page(5)
+        subtract(7)
+        make_x(5, x_rows[1][:, 1, :])
+        nc.sync.dma_start(staged_pair[:, 1, :], pages[5][:])
+        interleave(x_bf[1], x_rows[1][:], 0)
+        for n in range(pieces):
+            interleave(page_bf[1][n], staged_pair[:, :, n * PIECE : (n + 1) * PIECE], 0)
+
+        scatter(6)
+        quantize_page(0, 2)
+        make_tanh(7, page_home[0][2])
+        quantize_page(0, 3)
+        quantize_x(0)
+        make_factor(7, shared[0])
+        for n in range(pieces):
+            round_page_slice(6, n)
+        gather_page(6, page_home[0][3])
+        make_x(6, x_bf[1][:, :, 2])
+        for c in range(MT // 2):
+            open_sums(c)
+
+        scatter(7)
+        for n in range(pieces):
+            round_page_slice(7, n)
+        gather_page(7)
+        quantize_page(1, 0)
+        make_x(7, x_bf[1][:, :, 3])
+        quantize_page(1, 1)
+        quantize_x(1)
+        quantize_page(1, 2)
+        quantize_page(1, 3)
+        for c in range(MT // 2):
+            second_pass(f_sum[c], c, 1, q_w, q_s)
+        for c in range(MT // 2):
+            second_pass(e_sum[c], c, 1, x_w, x_s)
+
+        def finish(c):
+            f_sb = ringed([P, NP], F32, "f_sb%d" % c, ("lesser", "diff")[c % 2], 2)
+            nc.scalar.copy(f_sb[:], f_sum[c][:])
+            product = raw_tile([P, NP], "product%d" % c)
+            nc.vector.tensor_tensor(product[:], e_sum[c][:], f_sb[:], ALU.mult)
+            if c < PACK:
+                result = kept([P, NP], F32, "result%d" % c, "wgs_t%d" % c)
+            else:
+                result = ringed([P, NP], F32, "result%d" % c, "cap", 4)
+            slot_c = slot_t[:, c : c + 1]
+            if c < MT - 2:
+                nc.gpsimd.tensor_scalar(result[:], product[:], 1.0, slot_c, ALU.mult, ALU.add)
+            elif c == MT - 2:
+                nc.scalar.activation(result[:], product[:], ACT.Identity, bias=slot_c)
+            else:
+                nc.vector.tensor_scalar(result[:], product[:], slot_c, None, ALU.add)
+            nc.sync.dma_start(out[c * P : (c + 1) * P, :], result[:])
+
+        for c in range(MT):
+            finish(c)
+            if c + MT // 2 < MT:
+                later = c + MT // 2
+                f_sum[later] = bank(2 * c, "f_sum%d" % later)
+                e_sum[later] = bank(2 * c + 1, "e_sum%d" % later)
+                for b in range(HB):
+                    second_pass(f_sum[later], later, b, q_w, q_s)
+                for b in range(HB):
+                    second_pass(e_sum[later], later, b, x_w, x_s)

@@ -43,7 +43,7 @@ def tile_list_darts_slot_scores_kernel(
             return ring.tile(shape, dtype, name=name, tag=tag, bufs=bufs, align_bytes=64)
 
         def raw_tile(shape, name):
-            return ringed(shape, F32, name, "raw", 4)
+            return ringed(shape, F32, name, "raw", 5)
 
         def bank(n, name):
             return psum.tile([P, 512], F32, name=name, tag="bank%d" % n)
@@ -85,7 +85,7 @@ def tile_list_darts_slot_scores_kernel(
         caps, pages = {}, {}
 
         def load_cap(i):
-            caps[i] = ringed([P, S], F32, "cap%d" % i, "cap", 4)
+            caps[i] = kept([P, S], F32, "cap%d" % i)
             nc.sync.dma_start(caps[i][:], cap_rows[i // PACK][i % PACK])
 
         def load_page(i):
@@ -93,24 +93,28 @@ def tile_list_darts_slot_scores_kernel(
             nc.sync.dma_start(pages[i][:], page_rows[i // PACK][i % PACK])
 
         nc.sync.dma_start(idx[:], offs)
-        load_tab(0)
-        for quad in range(4):
-            rows = tab_scales[:, 4 * quad : 4 * quad + 4, :].rearrange("a r n -> r a n")
-            nc.sync.dma_start(tab_s[32 * quad : 32 * quad + 4].bitcast(I32), rows.bitcast(I32))
-        for quad in range(4):
-            rows = w4_scales[:, 4 * quad : 4 * quad + 4, :].rearrange("a r n -> r a n")
-            nc.sync.dma_start(w4_s_raw[32 * quad : 32 * quad + 4].bitcast(I32), rows.bitcast(I32))
-        for row, vector in enumerate((gain, lows, vec)):
-            nc.sync.dma_start(vectors[row:P:32], vector.rearrange("(b g c) -> g b c", b=HB, g=4))
+        first_words = tab_words[0].rearrange("p n i -> p (n i)").bitcast(I32)
+        for half in range(2):
+            cols = slice(half * (T // 2), (half + 1) * (T // 2))
+            nc.sync.dma_start(tab_w[0][:, cols], first_words[:, cols])
+        nc.sync.dma_start(idx2[:], offs2)
+        nc.sync.dma_start(idx3[:], offs3)
+        for raw_scales, scales in ((tab_s, tab_scales), (w4_s_raw, w4_scales)):
+            rows = scales.rearrange("a (g r) n -> r g a n", r=4).bitcast(I32)
+            for r in range(4):
+                nc.sync.dma_start(raw_scales[r:P:32].bitcast(I32), rows[r])
         w4_raw = kept([P, KA, H // 2], I32, "w4_raw")
         nc.sync.dma_start(w4_raw[:], w4_words.rearrange("a p n -> p a n").bitcast(I32))
         w1_raw = {}
         w1_raw[0, 0] = load_w1(0, 0, KP)
-        load_tab(1)
         w1_raw[1, 0] = load_w1(1, 0, KP)
+        load_tab(1)
+        w1_raw[2, 0] = load_w1(2, 0, KP)
         load_tab(2)
-        w1_last = [load_w1(2, half * (KP // 2), KP // 2) for half in range(2)]
-        load_cap(0)
+        for i in range(PACK):
+            load_cap(i)
+        for row, vector in enumerate((gain, lows, vec)):
+            nc.sync.dma_start(vectors[row:P:32], vector.rearrange("(b g c) -> g b c", b=HB, g=4))
         wgs_rows = wgs.rearrange("(u t e) s -> t u e s", t=PACK, e=RUN)
         wgs_t = [kept([P, S], F32, "wgs_t%d" % t) for t in range(PACK)]
 
@@ -118,17 +122,13 @@ def tile_list_darts_slot_scores_kernel(
             for quad in range(4):
                 nc.sync.dma_start(wgs_t[t][32 * quad : 32 * quad + 32], wgs_rows[t])
 
-        load_wgs(0)
-        nc.sync.dma_start(idx2[:], offs2)
-        load_cap(1)
-        load_page(0)
-        nc.sync.dma_start(idx3[:], offs3)
-        load_page(1)
-        load_wgs(1)
-        load_cap(2)
-        load_wgs(2)
-        load_cap(3)
-        load_wgs(3)
+        for t in range(PACK):
+            load_wgs(t)
+            load_page(t)
+        for a in range(KA):
+            w1_raw[a, 1] = load_w1(a, KP, KP)
+        load_cap(4)
+        load_cap(5)
 
         v_w = [kept([P, S], U32, "v_w%d" % a) for a in range(KA)]
         v_s = [kept([P, S], U8, "v_s%d" % a) for a in range(KA)]
@@ -160,40 +160,32 @@ def tile_list_darts_slot_scores_kernel(
         nc.vector.transpose(per_row[:], vectors_dealt[:])
 
         w1_w, w1_s = {}, {}
-        shared = [kept([P, KP * PACK // 2], F32, "shared%d" % b) for b in range(HB)]
-
-        def rounded_tile(name):
-            return ringed([P, KP * PACK], BF16, name, "rounded", 2)
+        homes = [kept([P, KP * PACK // 2], F32, "home%d" % a) for a in range(KA)]
 
         def round_w1(a, b):
-            if (a, b) == (KA - 1, HB - 1):
-                rounded = shared[0][:].bitcast(BF16)
-            else:
-                rounded = rounded_tile("w1_bf%d_%d" % (a, b))[:]
             nc.scalar.copy(
-                rounded.rearrange("p (t u e j) -> p u t j e", t=PACK, e=RUN, j=PACK),
+                homes[a][:].bitcast(BF16).rearrange("p (t u e j) -> p u t j e", t=PACK, e=RUN, j=PACK),
                 w1_raw[a, b][:].rearrange("p j (u t e) -> p u t j e", t=PACK, e=RUN),
             )
-            return rounded
 
-        def quantize_w1(a, b, rounded):
+        def quantize_w1(a, b):
             w1_w[a, b] = kept([P, KP], U32, "w1_w%d_%d" % (a, b))
             w1_s[a, b] = kept([P, KP], U8, "w1_s%d_%d" % (a, b))
-            quantize(w1_w[a, b][:], w1_s[a, b][:], rounded)
+            quantize(w1_w[a, b][:], w1_s[a, b][:], homes[a][:].bitcast(BF16))
 
-        rounded = round_w1(0, 0)
+        round_w1(0, 0)
+        quantize_w1(0, 0)
+        round_w1(1, 0)
         gather_words(1)
-        quantize_w1(0, 0, rounded)
-        rounded = round_w1(1, 0)
+        quantize_w1(1, 0)
+        raw_halves = w1_raw[2, 0][:].rearrange("p j (h u t e) -> p h u t j e", h=2, t=PACK, e=RUN)
+        halves = homes[2][:].bitcast(BF16).rearrange("p (t h u e j) -> p h u t j e", t=PACK, h=2, e=RUN, j=PACK)
+        nc.scalar.copy(halves[:, 0], raw_halves[:, 0])
+        nc.vector.tensor_copy(halves[:, 1], raw_halves[:, 1])
+        quantize_w1(2, 0)
         gather_words(2)
-        quantize_w1(1, 0, rounded)
-        rounded = rounded_tile("w1_bf2_0")[:]
-        halves = rounded.rearrange("p (t h u e j) -> p h u t j e", t=PACK, h=2, e=RUN, j=PACK)
-        nc.scalar.copy(halves[:, 0], w1_last[0][:].rearrange("p j (u t e) -> p u t j e", t=PACK, e=RUN))
-        nc.vector.tensor_copy(halves[:, 1], w1_last[1][:].rearrange("p j (u t e) -> p u t j e", t=PACK, e=RUN))
-        quantize_w1(2, 0, rounded)
 
-        sums, lesser, tanhs, factors, picked = {}, {}, {}, {}, {}
+        sums, lesser, factors, picked = {}, {}, {}, {}
 
         def first_products(i):
             b, t = divmod(i, PACK)
@@ -201,15 +193,6 @@ def tile_list_darts_slot_scores_kernel(
             b_sum = bank((2 * i + 1) % 8, "b_sum%d" % i)
             cols = slice(t * P, (t + 1) * P)
             for a in range(KA):
-                nc.tensor.matmul_mx(
-                    out=b_sum[:],
-                    lhsT=w4_w[:, a * HB + b, t, :].bitcast(FP4X4),
-                    lhsT_scale=w4_s[:, a * HB + b, t, :],
-                    rhs=v_w[a][:].bitcast(FP8X4),
-                    rhs_scale=v_s[a][:],
-                    start=(a == 0),
-                    stop=(a == KA - 1),
-                )
                 nc.tensor.matmul_mx(
                     out=a_sum[:],
                     lhsT=w1_w[a, b][:, cols].bitcast(FP8X4),
@@ -219,31 +202,37 @@ def tile_list_darts_slot_scores_kernel(
                     start=(a == 0),
                     stop=(a == KA - 1),
                 )
+                nc.tensor.matmul_mx(
+                    out=b_sum[:],
+                    lhsT=w4_w[:, a * HB + b, t, :].bitcast(FP4X4),
+                    lhsT_scale=w4_s[:, a * HB + b, t, :],
+                    rhs=v_w[a][:].bitcast(FP8X4),
+                    rhs_scale=v_s[a][:],
+                    start=(a == 0),
+                    stop=(a == KA - 1),
+                )
             sums[i] = (a_sum, b_sum)
 
-        def take_min(i):
-            lesser[i] = ringed([P, S], F32, "lesser%d" % i, "lesser", 2)
-            nc.vector.tensor_tensor(lesser[i][:], sums[i][0][:], caps[i][:], ALU.min)
+        def take_min(i, home=None):
+            lesser[i] = caps[i][:] if home is None else home
+            nc.vector.tensor_tensor(lesser[i], sums[i][0][:], caps[i][:], ALU.min)
 
-        diffs = {}
+        def subtract_and_tanh(i, home=None):
+            diff = caps[i][:] if home is None else home
+            nc.vector.tensor_tensor(diff, sums[i][1][:], lesser[i], ALU.subtract)
+            nc.scalar.activation(caps[i][:], diff, ACT.Tanh)
 
-        def subtract(i):
-            diffs[i] = ringed([P, S], F32, "diff%d" % i, "diff", 2)
-            nc.vector.tensor_tensor(diffs[i][:], sums[i][1][:], lesser[i][:], ALU.subtract)
-
-        def make_factor(i, home=None):
-            factors[i] = ringed([P, S], F32, "factor%d" % i, "factor", 3)[:] if home is None else home[:, 0:S]
-            nc.scalar.activation(factors[i], wgs_t[i % PACK][:], ACT.Copy, scale=per_row[:, 32 * i : 32 * i + 1])
-
-        def make_tanh(i, home=None):
-            tanhs[i] = ringed([P, S], F32, "tanh%d" % i, "tanh", 3)[:] if home is None else home[:, 0:S]
-            nc.scalar.activation(tanhs[i], diffs[i][:], ACT.Tanh)
+        def make_factors(t):
+            factors[t] = kept([P, S], F32, "factor%d" % t)
+            factors[t + PACK] = wgs_t[t]
+            for i in (t, t + PACK):
+                nc.scalar.activation(factors[i][:], wgs_t[t][:], ACT.Copy, scale=per_row[:, 32 * i : 32 * i + 1])
 
         def scatter(i):
-            nc.vector.tensor_tensor(pages[i][:].indirect(idx2[:]), tanhs[i], factors[i], ALU.mult)
+            nc.vector.tensor_tensor(pages[i][:].indirect(idx2[:]), caps[i][:], factors[i][:], ALU.mult)
 
         def gather_page(i, home=None):
-            picked[i] = ringed([P, NP], F32, "picked%d" % i, "picked", 2)[:] if home is None else home[:, 0:NP]
+            picked[i] = ringed([P, NP], F32, "picked%d" % i, "picked", 2)[:] if home is None else home
             nc.vector.tensor_copy(picked[i], pages[i][:].indirect(idx3[:]))
 
         def make_x(i, target):
@@ -259,7 +248,8 @@ def tile_list_darts_slot_scores_kernel(
             )
 
         x_rows = [kept([P, PACK, NP], BF16, "x_rows0"), kept([P, 2, NP], BF16, "x_rows1")]
-        x_bf = [shared[b][:].bitcast(BF16).rearrange("p (n t) -> p n t", t=PACK) for b in range(HB)]
+        x_home = [homes[2], homes[0]]
+        x_bf = [x_home[b][:].bitcast(BF16).rearrange("p (n t) -> p n t", t=PACK) for b in range(HB)]
         x_w = [kept([P, NP], U32, "x_w%d" % b) for b in range(HB)]
         x_s = [kept([P, NP], U8, "x_s%d" % b) for b in range(HB)]
         q_w = [kept([P, NP], U32, "q_w%d" % b) for b in range(HB)]
@@ -271,18 +261,16 @@ def tile_list_darts_slot_scores_kernel(
         page_s = [[kept([P, PIECE], U8, "page_s%d_%d" % (b, n)) for n in range(pieces)] for b in range(HB)]
 
         def quantize_x(b):
-            quantize(x_w[b][:], x_s[b][:], shared[b][:].bitcast(BF16))
+            quantize(x_w[b][:], x_s[b][:], x_home[b][:].bitcast(BF16))
 
         def quantize_page(b, n):
             quantize(page_w[b][n][:], page_s[b][n][:], page_home[b][n][:].bitcast(BF16))
 
         def round_q(b, raw):
-            if b == 0:
-                rounded_q = rounded_tile("q_bf0")[:]
-            else:
-                rounded_q = shared[1][:].bitcast(BF16)
-            interleave(rounded_q.rearrange("p (n t) -> p n t", t=PACK), raw[:], 0)
-            return rounded_q
+            interleave(homes[b][:].bitcast(BF16).rearrange("p (n t) -> p n t", t=PACK), raw[:], 0)
+
+        def quantize_q(b):
+            quantize(q_w[b][:], q_s[b][:], homes[b][:].bitcast(BF16))
 
         def round_page_slice(i, n):
             b, t = divmod(i, PACK)
@@ -303,72 +291,34 @@ def tile_list_darts_slot_scores_kernel(
                 stop=(b == HB - 1),
             )
 
-        def open_sums(c):
-            f_sum[c] = bank(2 * c % 8, "f_sum%d" % c)
-            e_sum[c] = bank((2 * c + 1) % 8, "e_sum%d" % c)
-            second_pass(f_sum[c], c, 0, q_w, q_s)
-            second_pass(e_sum[c], c, 0, x_w, x_s)
-
-        def min_of(i):
-            if i >= PACK:
-                first_products(i)
-            take_min(i)
-
         def load_q(b):
             raw = raw_tile([P, PACK, NP], "q_raw%d" % b)
             for t in range(PACK):
                 nc.sync.dma_start(raw[:, t, :], q_rows[b][t])
             return raw
 
-        for i in range(PACK):
-            first_products(i)
-        take_min(0)
-        subtract(0)
-        make_factor(0)
-        make_tanh(0)
-        take_min(1)
-        subtract(1)
-        make_factor(1)
-        make_tanh(1)
-
-        w1_raw[0, 1] = load_w1(0, KP, KP)
-        w1_raw[1, 1] = load_w1(1, KP, KP)
-        load_page(2)
-        w1_raw[2, 1] = load_w1(2, KP, KP)
-
-        scatter(0)
-        min_of(2)
-        gather_page(0)
-        subtract(2)
-        make_x(0, x_rows[0][:, 0, :])
-        make_factor(2)
-        make_tanh(2)
-        load_cap(4)
-        load_page(3)
         q_raw = [load_q(0)]
-
-        rounded = round_w1(0, 1)
-        scatter(1)
-        quantize_w1(0, 1, rounded)
-        min_of(3)
-        gather_page(1)
-        subtract(3)
-        make_x(1, x_rows[0][:, 1, :])
-        make_tanh(3)
-        load_cap(5)
         load_page(4)
         q_raw.append(load_q(1))
-
-        rounded = round_w1(1, 1)
-        rounded_last = round_w1(2, 1)
-        scatter(2)
-        quantize_w1(1, 1, rounded)
-        quantize_w1(2, 1, rounded_last)
-        make_factor(3, shared[0])
-        gather_page(2)
-        make_x(2, x_rows[0][:, 2, :])
-        load_cap(6)
         load_page(5)
+
+        for i in range(PACK):
+            first_products(i)
+        for i in range(PACK):
+            take_min(i)
+            make_factors(i)
+            subtract_and_tanh(i)
+        scatter(0)
+        scatter(1)
+        gather_page(0)
+        scatter(2)
+        make_x(0, x_rows[0][:, 0, :])
+        scatter(3)
+        staged = [raw_tile([P, PACK, T2 // 2], "staged%d" % half) for half in range(2)]
+        for half in range(2):
+            for t in range(PACK):
+                nc.sync.dma_start(staged[half][:, t, :], pages[t][:, half * (T2 // 2) : (half + 1) * (T2 // 2)])
+        load_cap(6)
         load_cap(7)
         load_page(6)
         load_page(7)
@@ -376,104 +326,87 @@ def tile_list_darts_slot_scores_kernel(
         with nc.allow_non_contiguous_dma(reason="one value of slot for each output row"):
             nc.sync.dma_start(slot_t[:], slot.rearrange("(c p) -> p c", p=P))
 
-        q_bf = [round_q(0, q_raw[0])]
-        scatter(3)
-        min_of(4)
-        gather_page(3)
-        subtract(4)
+        for a in range(KA):
+            round_w1(a, 1)
+            quantize_w1(a, 1)
+        round_q(0, q_raw[0])
+        round_q(1, q_raw[1])
+        gather_page(1, homes[2][:, 0:NP])
+        gather_page(2, homes[2][:, NP : 2 * NP])
+        make_x(1, x_rows[0][:, 1, :])
+        make_x(2, x_rows[0][:, 2, :])
+        gather_page(3, homes[2][:, 0:NP])
+        for i in range(PACK, SLICES):
+            first_products(i)
+        take_min(4)
         make_x(3, x_rows[0][:, 3, :])
-        make_factor(4)
-        make_tanh(4)
-        min_of(5)
-        quantize(q_w[0][:], q_s[0][:], q_bf[0])
-        subtract(5)
-        make_tanh(5)
-        staged = [raw_tile([P, PACK, T2 // 2], "staged%d" % half) for half in range(2)]
-        for half in range(2):
-            for t in range(PACK):
-                nc.sync.dma_start(staged[half][:, t, :], pages[t][:, half * (T2 // 2) : (half + 1) * (T2 // 2)])
-        q_bf.append(round_q(1, q_raw[1]))
-
-        scatter(4)
-        quantize(q_w[1][:], q_s[1][:], q_bf[1])
-        make_factor(5, shared[1])
-        min_of(6)
-        gather_page(4)
-        subtract(6)
-        make_x(4, x_rows[1][:, 0, :])
-        make_tanh(6)
-        interleave(x_bf[0], x_rows[0][:], 0)
+        take_min(5)
+        subtract_and_tanh(4)
+        subtract_and_tanh(5)
+        quantize_q(0)
         for n in range(pieces):
             interleave(page_bf[0][n], staged[n // 2][:, :, n % 2 * PIECE : (n % 2 + 1) * PIECE], 0)
-        staged_pair = raw_tile([P, 2, T2], "staged_pair")
-        nc.sync.dma_start(staged_pair[:, 0, :], pages[4][:])
+        interleave(x_bf[0], x_rows[0][:], 0)
 
-        scatter(5)
+        staged_pair = raw_tile([P, 2, T2], "staged_pair")
+        for t in range(2):
+            scatter(PACK + t)
+            nc.sync.dma_start(staged_pair[:, t, :], pages[PACK + t][:])
+        gather_page(4)
         quantize_page(0, 0)
         quantize_page(0, 1)
-        make_factor(6, page_home[0][1])
-        min_of(7)
         gather_page(5)
-        subtract(7)
+        make_x(4, x_rows[1][:, 0, :])
         make_x(5, x_rows[1][:, 1, :])
-        nc.sync.dma_start(staged_pair[:, 1, :], pages[5][:])
-        interleave(x_bf[1], x_rows[1][:], 0)
+        quantize_x(0)
+        quantize_q(1)
         for n in range(pieces):
             interleave(page_bf[1][n], staged_pair[:, :, n * PIECE : (n + 1) * PIECE], 0)
+        take_min(6, staged_pair[:, 0, 0:S])
+        take_min(7, staged_pair[:, 1, 0:S])
+        subtract_and_tanh(6)
+        subtract_and_tanh(7, homes[0][:, 0:S])
+        interleave(x_bf[1], x_rows[1][:], 0)
 
-        scatter(6)
-        quantize_page(0, 2)
-        make_tanh(7, page_home[0][2])
-        quantize_page(0, 3)
-        quantize_x(0)
-        make_factor(7, shared[0])
-        for n in range(pieces):
-            round_page_slice(6, n)
-        gather_page(6, page_home[0][3])
-        make_x(6, x_bf[1][:, :, 2])
+        def open_f(c):
+            f_sum[c] = bank(c, "f_sum%d" % c)
+            second_pass(f_sum[c], c, 0, q_w, q_s)
+
         for c in range(MT // 2):
-            open_sums(c)
-
-        scatter(7)
-        for n in range(pieces):
-            round_page_slice(7, n)
-        gather_page(7)
+            open_f(c)
+        for i in (6, 7):
+            scatter(i)
+            for n in range(pieces):
+                round_page_slice(i, n)
+        late_w = kept([P, 2 * PIECE], U32, "late_w", "wgs_t2")
+        for n in (2, 3):
+            page_w[0][n] = late_w[:, (n - 2) * PIECE : (n - 1) * PIECE]
+            quantize_page(0, n)
+        for c in range(MT // 2, MT):
+            open_f(c)
+        gather_page(6)
+        make_x(6, x_bf[1][:, :, 2])
         quantize_page(1, 0)
-        make_x(7, x_bf[1][:, :, 3])
         quantize_page(1, 1)
-        quantize_x(1)
+        gather_page(7, page_home[1][0][:])
         quantize_page(1, 2)
         quantize_page(1, 3)
-        for c in range(MT // 2):
+        make_x(7, x_bf[1][:, :, 3])
+        quantize_x(1)
+        for c in range(MT):
             second_pass(f_sum[c], c, 1, q_w, q_s)
-        for c in range(MT // 2):
-            second_pass(e_sum[c], c, 1, x_w, x_s)
-
-        def finish(c):
-            f_sb = ringed([P, NP], F32, "f_sb%d" % c, ("lesser", "diff")[c % 2], 2)
-            nc.scalar.copy(f_sb[:], f_sum[c][:])
-            product = raw_tile([P, NP], "product%d" % c)
-            nc.vector.tensor_tensor(product[:], e_sum[c][:], f_sb[:], ALU.mult)
-            if c < PACK:
-                result = kept([P, NP], F32, "result%d" % c, "wgs_t%d" % c)
-            else:
-                result = ringed([P, NP], F32, "result%d" % c, "cap", 4)
-            slot_c = slot_t[:, c : c + 1]
-            if c < MT - 2:
-                nc.gpsimd.tensor_scalar(result[:], product[:], 1.0, slot_c, ALU.mult, ALU.add)
-            elif c == MT - 2:
-                nc.scalar.activation(result[:], product[:], ACT.Identity, bias=slot_c)
-            else:
-                nc.vector.tensor_scalar(result[:], product[:], slot_c, None, ALU.add)
-            nc.sync.dma_start(out[c * P : (c + 1) * P, :], result[:])
+            nc.scalar.copy(caps[c][:], f_sum[c][:])
+            e_sum[c] = bank(c, "e_sum%d" % c)
+            second_pass(e_sum[c], c, 0, x_w, x_s)
 
         for c in range(MT):
-            finish(c)
-            if c + MT // 2 < MT:
-                later = c + MT // 2
-                f_sum[later] = bank(2 * c, "f_sum%d" % later)
-                e_sum[later] = bank(2 * c + 1, "e_sum%d" % later)
-                for b in range(HB):
-                    second_pass(f_sum[later], later, b, q_w, q_s)
-                for b in range(HB):
-                    second_pass(e_sum[later], later, b, x_w, x_s)
+            second_pass(e_sum[c], c, 1, x_w, x_s)
+            nc.vector.tensor_tensor(caps[c][:], e_sum[c][:], caps[c][:], ALU.mult)
+            slot_c = slot_t[:, c : c + 1]
+            if c % 2 == 0:
+                nc.scalar.activation(caps[c][:], caps[c][:], ACT.Identity, bias=slot_c)
+            elif c < MT - 1:
+                nc.gpsimd.tensor_scalar(caps[c][:], caps[c][:], 1.0, slot_c, ALU.mult, ALU.add)
+            else:
+                nc.vector.tensor_scalar(caps[c][:], caps[c][:], slot_c, None, ALU.add)
+            nc.sync.dma_start(out[c * P : (c + 1) * P, :], caps[c][:])

@@ -107,14 +107,14 @@ def tile_list_darts_slot_scores_kernel(
         nc.sync.dma_start(w4_raw[:], w4_words.rearrange("a p n -> p a n").bitcast(I32))
         w1_raw = {}
         w1_raw[0, 0] = load_w1(0, 0, KP)
-        w1_raw[1, 0] = load_w1(1, 0, KP)
         load_tab(1)
+        for row, vector in enumerate((gain, lows, vec)):
+            nc.sync.dma_start(vectors[row:P:32], vector.rearrange("(b g c) -> g b c", b=HB, g=4))
+        w1_raw[1, 0] = load_w1(1, 0, KP)
         w1_raw[2, 0] = load_w1(2, 0, KP)
         load_tab(2)
         for i in range(PACK):
             load_cap(i)
-        for row, vector in enumerate((gain, lows, vec)):
-            nc.sync.dma_start(vectors[row:P:32], vector.rearrange("(b g c) -> g b c", b=HB, g=4))
         wgs_rows = wgs.rearrange("(u t e) s -> t u e s", t=PACK, e=RUN)
         wgs_t = [kept([P, S], F32, "wgs_t%d" % t) for t in range(PACK)]
 
@@ -122,11 +122,16 @@ def tile_list_darts_slot_scores_kernel(
             for quad in range(4):
                 nc.sync.dma_start(wgs_t[t][32 * quad : 32 * quad + 32], wgs_rows[t])
 
-        for t in range(PACK):
+        for t in range(2):
             load_wgs(t)
             load_page(t)
-        for a in range(KA):
-            w1_raw[a, 1] = load_w1(a, KP, KP)
+        w1_raw[0, 1] = load_w1(0, KP, KP)
+        load_wgs(2)
+        load_page(2)
+        w1_raw[1, 1] = load_w1(1, KP, KP)
+        load_wgs(3)
+        w1_raw[2, 1] = load_w1(2, KP, KP)
+        load_page(3)
         load_cap(4)
         load_cap(5)
 
@@ -173,16 +178,18 @@ def tile_list_darts_slot_scores_kernel(
             w1_s[a, b] = kept([P, KP], U8, "w1_s%d_%d" % (a, b))
             quantize(w1_w[a, b][:], w1_s[a, b][:], homes[a][:].bitcast(BF16))
 
+        def round_w1_shared(a):
+            raw_halves = w1_raw[a, 0][:].rearrange("p j (h u t e) -> p h u t j e", h=2, t=PACK, e=RUN)
+            halves = homes[a][:].bitcast(BF16).rearrange("p (t h u e j) -> p h u t j e", t=PACK, h=2, e=RUN, j=PACK)
+            nc.scalar.copy(halves[:, 0], raw_halves[:, 0])
+            nc.vector.tensor_copy(halves[:, 1], raw_halves[:, 1])
+
         round_w1(0, 0)
-        quantize_w1(0, 0)
-        round_w1(1, 0)
         gather_words(1)
-        quantize_w1(1, 0)
-        raw_halves = w1_raw[2, 0][:].rearrange("p j (h u t e) -> p h u t j e", h=2, t=PACK, e=RUN)
-        halves = homes[2][:].bitcast(BF16).rearrange("p (t h u e j) -> p h u t j e", t=PACK, h=2, e=RUN, j=PACK)
-        nc.scalar.copy(halves[:, 0], raw_halves[:, 0])
-        nc.vector.tensor_copy(halves[:, 1], raw_halves[:, 1])
-        quantize_w1(2, 0)
+        quantize_w1(0, 0)
+        for a in range(1, KA):
+            round_w1_shared(a)
+            quantize_w1(a, 0)
         gather_words(2)
 
         sums, lesser, factors, picked = {}, {}, {}, {}
@@ -248,11 +255,15 @@ def tile_list_darts_slot_scores_kernel(
             )
 
         x_rows = [kept([P, PACK, NP], BF16, "x_rows0"), kept([P, 2, NP], BF16, "x_rows1")]
-        x_home = [homes[2], homes[0]]
-        x_bf = [x_home[b][:].bitcast(BF16).rearrange("p (n t) -> p n t", t=PACK) for b in range(HB)]
+        x_home, x_bf = {}, {}
+
+        def house_x(b, home):
+            x_home[b] = home
+            x_bf[b] = home.bitcast(BF16).rearrange("p (n t) -> p n t", t=PACK)
+
         x_w = [kept([P, NP], U32, "x_w%d" % b) for b in range(HB)]
         x_s = [kept([P, NP], U8, "x_s%d" % b) for b in range(HB)]
-        q_w = [kept([P, NP], U32, "q_w%d" % b) for b in range(HB)]
+        q_w = {0: kept([P, NP], U32, "q_w0")}
         q_s = [kept([P, NP], U8, "q_s%d" % b) for b in range(HB)]
         pieces = T2 // PIECE
         page_home = [[kept([P, PIECE * PACK // 2], F32, "page_bf%d_%d" % (b, n)) for n in range(pieces)] for b in range(HB)]
@@ -261,7 +272,7 @@ def tile_list_darts_slot_scores_kernel(
         page_s = [[kept([P, PIECE], U8, "page_s%d_%d" % (b, n)) for n in range(pieces)] for b in range(HB)]
 
         def quantize_x(b):
-            quantize(x_w[b][:], x_s[b][:], x_home[b][:].bitcast(BF16))
+            quantize(x_w[b][:], x_s[b][:], x_home[b].bitcast(BF16))
 
         def quantize_page(b, n):
             quantize(page_w[b][n][:], page_s[b][n][:], page_home[b][n][:].bitcast(BF16))
@@ -297,9 +308,8 @@ def tile_list_darts_slot_scores_kernel(
                 nc.sync.dma_start(raw[:, t, :], q_rows[b][t])
             return raw
 
-        q_raw = [load_q(0)]
+        q_raw = [load_q(b) for b in range(HB)]
         load_page(4)
-        q_raw.append(load_q(1))
         load_page(5)
 
         for i in range(PACK):
@@ -346,6 +356,7 @@ def tile_list_darts_slot_scores_kernel(
         quantize_q(0)
         for n in range(pieces):
             interleave(page_bf[0][n], staged[n // 2][:, :, n % 2 * PIECE : (n % 2 + 1) * PIECE], 0)
+        house_x(0, staged[1][:, 0:2, :].rearrange("p t m -> p (t m)"))
         interleave(x_bf[0], x_rows[0][:], 0)
 
         staged_pair = raw_tile([P, 2, T2], "staged_pair")
@@ -359,13 +370,15 @@ def tile_list_darts_slot_scores_kernel(
         make_x(4, x_rows[1][:, 0, :])
         make_x(5, x_rows[1][:, 1, :])
         quantize_x(0)
+        q_w[1] = kept([P, NP], U32, "q_w1", "x_rows0")
         quantize_q(1)
         for n in range(pieces):
             interleave(page_bf[1][n], staged_pair[:, :, n * PIECE : (n + 1) * PIECE], 0)
-        take_min(6, staged_pair[:, 0, 0:S])
-        take_min(7, staged_pair[:, 1, 0:S])
+        take_min(6, staged[1][:, 0, :])
+        take_min(7, staged[1][:, 1, :])
         subtract_and_tanh(6)
         subtract_and_tanh(7, homes[0][:, 0:S])
+        house_x(1, homes[0][:])
         interleave(x_bf[1], x_rows[1][:], 0)
 
         def open_f(c):
@@ -378,7 +391,7 @@ def tile_list_darts_slot_scores_kernel(
             scatter(i)
             for n in range(pieces):
                 round_page_slice(i, n)
-        late_w = kept([P, 2 * PIECE], U32, "late_w", "wgs_t2")
+        late_w = kept([P, 2 * PIECE], U32, "late_w", "wgs_t3")
         for n in (2, 3):
             page_w[0][n] = late_w[:, (n - 2) * PIECE : (n - 1) * PIECE]
             quantize_page(0, n)
@@ -390,23 +403,28 @@ def tile_list_darts_slot_scores_kernel(
         quantize_page(1, 1)
         gather_page(7, page_home[1][0][:])
         quantize_page(1, 2)
-        quantize_page(1, 3)
         make_x(7, x_bf[1][:, :, 3])
         quantize_x(1)
+        quantize_page(1, 3)
         for c in range(MT):
             second_pass(f_sum[c], c, 1, q_w, q_s)
             nc.scalar.copy(caps[c][:], f_sum[c][:])
+        for c in range(MT):
             e_sum[c] = bank(c, "e_sum%d" % c)
-            second_pass(e_sum[c], c, 0, x_w, x_s)
+            for b in range(HB):
+                second_pass(e_sum[c], c, b, x_w, x_s)
 
         for c in range(MT):
-            second_pass(e_sum[c], c, 1, x_w, x_s)
-            nc.vector.tensor_tensor(caps[c][:], e_sum[c][:], caps[c][:], ALU.mult)
             slot_c = slot_t[:, c : c + 1]
-            if c % 2 == 0:
-                nc.scalar.activation(caps[c][:], caps[c][:], ACT.Identity, bias=slot_c)
-            elif c < MT - 1:
-                nc.gpsimd.tensor_scalar(caps[c][:], caps[c][:], 1.0, slot_c, ALU.mult, ALU.add)
-            else:
-                nc.vector.tensor_scalar(caps[c][:], caps[c][:], slot_c, None, ALU.add)
-            nc.sync.dma_start(out[c * P : (c + 1) * P, :], caps[c][:])
+            parts = 1 if c < MT - 1 else 2
+            for part in range(parts):
+                cols = slice(part * NP // parts, (part + 1) * NP // parts)
+                result = caps[c][:, cols]
+                nc.vector.tensor_tensor(result, e_sum[c][:, cols], result, ALU.mult)
+                if c in (0, 1, 2, 4):
+                    nc.gpsimd.tensor_scalar(result, result, 1.0, slot_c, ALU.mult, ALU.add)
+                elif part == 0:
+                    nc.scalar.activation(result, result, ACT.Identity, bias=slot_c)
+                else:
+                    nc.vector.tensor_scalar(result, result, slot_c, None, ALU.add)
+                nc.sync.dma_start(out[c * P : (c + 1) * P, cols], result)

@@ -1,3 +1,4 @@
+import itertools
 from contextlib import ExitStack
 
 import concourse.mybir as mybir
@@ -23,7 +24,7 @@ KA = K // KP
 HB = H // KP
 SLICES = HB * PACK
 MT = T2 // P
-PIECE = 256
+PIECES = ((0, 256), (256, 256), (512, 512))
 RUN = 4
 
 
@@ -57,8 +58,9 @@ def tile_list_darts_slot_scores_kernel(
 
         tab_s = kept([P, KA, T], U8, "tab_s")
         w4_s_raw = kept([P, KA, H], U8, "w4_s_raw")
-        nc.vector.memset(tab_s[:].rearrange("p a n -> p (a n)").bitcast(I32), 0)
-        nc.vector.memset(w4_s_raw[:].rearrange("p a n -> p (a n)").bitcast(I32), 0)
+        v_s = kept([P, KA, S], U8, "v_s")
+        for engine, scales in ((nc.vector, tab_s), (nc.gpsimd, w4_s_raw), (nc.vector, v_s)):
+            engine.memset(scales[:].rearrange("p a n -> p (a n)").bitcast(I32), 0)
 
         vectors = kept([P, HB, P], F32, "vectors")
         nc.vector.memset(vectors[:], 0.0)
@@ -94,15 +96,18 @@ def tile_list_darts_slot_scores_kernel(
 
         nc.sync.dma_start(idx[:], offs)
         first_words = tab_words[0].rearrange("p n i -> p (n i)").bitcast(I32)
-        for half in range(2):
-            cols = slice(half * (T // 2), (half + 1) * (T // 2))
+
+        def load_first_words(part):
+            cols = slice(part * (T // 4), (part + 1) * (T // 4))
             nc.sync.dma_start(tab_w[0][:, cols], first_words[:, cols])
+
+        for part in range(3):
+            load_first_words(part)
         nc.sync.dma_start(idx2[:], offs2)
         nc.sync.dma_start(idx3[:], offs3)
-        for raw_scales, scales in ((tab_s, tab_scales), (w4_s_raw, w4_scales)):
-            rows = scales.rearrange("a (g r) n -> r g a n", r=4).bitcast(I32)
-            for r in range(4):
-                nc.sync.dma_start(raw_scales[r:P:32].bitcast(I32), rows[r])
+        for raw_scales, scales in ((w4_s_raw, w4_scales), (tab_s, tab_scales)):
+            nc.sync.dma_start(raw_scales[0:P:8].bitcast(I32), scales.rearrange("a g n -> g a n").bitcast(I32))
+        load_first_words(3)
         w4_raw = kept([P, KA, H // 2], I32, "w4_raw")
         nc.sync.dma_start(w4_raw[:], w4_words.rearrange("a p n -> p a n").bitcast(I32))
         w1_raw = {}
@@ -136,20 +141,23 @@ def tile_list_darts_slot_scores_kernel(
         load_cap(5)
 
         v_w = [kept([P, S], U32, "v_w%d" % a) for a in range(KA)]
-        v_s = [kept([P, S], U8, "v_s%d" % a) for a in range(KA)]
+        picked_s = kept([P, KA, S], U8, "picked_s")
 
         def gather_words(a):
             nc.vector.tensor_copy(v_w[a][:], tab_w[a][:].bitcast(U32).indirect(idx[:]))
-
-        gather_words(0)
-        for a in range(KA):
-            nc.vector.tensor_copy(v_s[a][:], tab_s[:, a, :].indirect(idx[:]))
 
         w4_s = kept([P, KA * HB, PACK, P], U8, "w4_s")
         nc.vector.tensor_copy(
             w4_s[:].bitcast(I32).rearrange("p g t u -> p g u t"),
             w4_s_raw[:].bitcast(I32).rearrange("p a (b u t) -> p (a b) u t", b=HB, t=PACK),
         )
+        for r in range(1, 4):
+            nc.gpsimd.dma_start(w4_s[r:P:32].bitcast(I32), w4_s[8 * r : P : 32].bitcast(I32))
+        for a in range(KA):
+            nc.vector.tensor_copy(picked_s[:, a, :], tab_s[:, a, :].indirect(idx[:]))
+        for r in range(4):
+            nc.gpsimd.dma_start(v_s[r:P:32].bitcast(I32), picked_s[8 * r : P : 32].bitcast(I32))
+        gather_words(0)
         w4_w = kept([P, KA * HB, PACK, P // 2], I32, "w4_w")
         nc.vector.tensor_copy(
             w4_w[:].rearrange("p g t (u e) -> p g u t e", e=2),
@@ -194,18 +202,19 @@ def tile_list_darts_slot_scores_kernel(
 
         sums, lesser, factors, picked = {}, {}, {}, {}
 
-        def first_products(i):
-            b, t = divmod(i, PACK)
-            a_sum = bank(2 * i % 8, "a_sum%d" % i)
-            b_sum = bank((2 * i + 1) % 8, "b_sum%d" % i)
-            cols = slice(t * P, (t + 1) * P)
-            for a in range(KA):
+        def first_products(b):
+            for t in range(PACK):
+                sums[b * PACK + t] = (bank(2 * t, "a_sum%d_%d" % (b, t)), bank(2 * t + 1, "b_sum%d_%d" % (b, t)))
+            order = list(itertools.product(range(KA), range(2))) + [(a, t) for t in range(2, PACK) for a in range(KA)]
+            for a, t in order:
+                a_sum, b_sum = sums[b * PACK + t]
+                cols = slice(t * P, (t + 1) * P)
                 nc.tensor.matmul_mx(
                     out=a_sum[:],
                     lhsT=w1_w[a, b][:, cols].bitcast(FP8X4),
                     lhsT_scale=w1_s[a, b][:, cols],
                     rhs=v_w[a][:].bitcast(FP8X4),
-                    rhs_scale=v_s[a][:],
+                    rhs_scale=v_s[:, a, :],
                     start=(a == 0),
                     stop=(a == KA - 1),
                 )
@@ -214,11 +223,10 @@ def tile_list_darts_slot_scores_kernel(
                     lhsT=w4_w[:, a * HB + b, t, :].bitcast(FP4X4),
                     lhsT_scale=w4_s[:, a * HB + b, t, :],
                     rhs=v_w[a][:].bitcast(FP8X4),
-                    rhs_scale=v_s[a][:],
+                    rhs_scale=v_s[:, a, :],
                     start=(a == 0),
                     stop=(a == KA - 1),
                 )
-            sums[i] = (a_sum, b_sum)
 
         def take_min(i, home=None):
             lesser[i] = caps[i][:] if home is None else home
@@ -229,11 +237,12 @@ def tile_list_darts_slot_scores_kernel(
             nc.vector.tensor_tensor(diff, sums[i][1][:], lesser[i], ALU.subtract)
             nc.scalar.activation(caps[i][:], diff, ACT.Tanh)
 
-        def make_factors(t):
+        for t in range(PACK):
             factors[t] = kept([P, S], F32, "factor%d" % t)
             factors[t + PACK] = wgs_t[t]
-            for i in (t, t + PACK):
-                nc.scalar.activation(factors[i][:], wgs_t[t][:], ACT.Copy, scale=per_row[:, 32 * i : 32 * i + 1])
+
+        def make_factor(i):
+            nc.scalar.activation(factors[i][:], wgs_t[i % PACK][:], ACT.Copy, scale=per_row[:, 32 * i : 32 * i + 1])
 
         def scatter(i):
             nc.vector.tensor_tensor(pages[i][:].indirect(idx2[:]), caps[i][:], factors[i][:], ALU.mult)
@@ -265,17 +274,21 @@ def tile_list_darts_slot_scores_kernel(
         x_s = [kept([P, NP], U8, "x_s%d" % b) for b in range(HB)]
         q_w = {0: kept([P, NP], U32, "q_w0")}
         q_s = [kept([P, NP], U8, "q_s%d" % b) for b in range(HB)]
-        pieces = T2 // PIECE
-        page_home = [[kept([P, PIECE * PACK // 2], F32, "page_bf%d_%d" % (b, n)) for n in range(pieces)] for b in range(HB)]
+        pieces = len(PIECES)
+        page_home = [[kept([P, PIECES[n][1] * PACK // 2], F32, "page_bf%d_%d" % (b, n)) for n in range(pieces)] for b in range(HB)]
         page_bf = [[home[:].bitcast(BF16).rearrange("p (n t) -> p n t", t=PACK) for home in homes] for homes in page_home]
-        page_w = [[kept([P, PIECE], U32, "page_w%d_%d" % (b, n)) for n in range(pieces)] for b in range(HB)]
-        page_s = [[kept([P, PIECE], U8, "page_s%d_%d" % (b, n)) for n in range(pieces)] for b in range(HB)]
+        page_w = {}
+        page_s = [[kept([P, PIECES[n][1]], U8, "page_s%d_%d" % (b, n)) for n in range(pieces)] for b in range(HB)]
+
+        def columns(n):
+            return slice(PIECES[n][0], PIECES[n][0] + PIECES[n][1])
 
         def quantize_x(b):
             quantize(x_w[b][:], x_s[b][:], x_home[b].bitcast(BF16))
 
-        def quantize_page(b, n):
-            quantize(page_w[b][n][:], page_s[b][n][:], page_home[b][n][:].bitcast(BF16))
+        def quantize_page(b, n, tag=None):
+            page_w[b, n] = kept([P, PIECES[n][1]], U32, "page_w%d_%d" % (b, n), tag)
+            quantize(page_w[b, n][:], page_s[b][n][:], page_home[b][n][:].bitcast(BF16))
 
         def round_q(b, raw):
             interleave(homes[b][:].bitcast(BF16).rearrange("p (n t) -> p n t", t=PACK), raw[:], 0)
@@ -285,16 +298,17 @@ def tile_list_darts_slot_scores_kernel(
 
         def round_page_slice(i, n):
             b, t = divmod(i, PACK)
-            nc.scalar.copy(page_bf[b][n][:, :, t], pages[i][:, n * PIECE : (n + 1) * PIECE])
+            nc.scalar.copy(page_bf[b][n][:, :, t], pages[i][:, columns(n)])
 
         q_rows = q.rearrange("(b u t e) s -> b t u e s", b=HB, t=PACK, e=RUN)
         e_sum, f_sum = {}, {}
 
         def second_pass(acc, c, b, moving_w, moving_s):
-            n, cols = c // 2, slice(c % 2 * P, (c % 2 + 1) * P)
+            n = min(c // 2, pieces - 1)
+            cols = slice(c * P - PIECES[n][0], (c + 1) * P - PIECES[n][0])
             nc.tensor.matmul_mx(
                 out=acc[:],
-                lhsT=page_w[b][n][:, cols].bitcast(FP8X4),
+                lhsT=page_w[b, n][:, cols].bitcast(FP8X4),
                 lhsT_scale=page_s[b][n][:, cols],
                 rhs=moving_w[b][:].bitcast(FP8X4),
                 rhs_scale=moving_s[b][:],
@@ -312,12 +326,11 @@ def tile_list_darts_slot_scores_kernel(
         load_page(4)
         load_page(5)
 
+        first_products(0)
         for i in range(PACK):
-            first_products(i)
-        for i in range(PACK):
-            take_min(i)
-            make_factors(i)
+            take_min(i, factors[i][:])
             subtract_and_tanh(i)
+            make_factor(i)
         scatter(0)
         scatter(1)
         gather_page(0)
@@ -339,6 +352,8 @@ def tile_list_darts_slot_scores_kernel(
         for a in range(KA):
             round_w1(a, 1)
             quantize_w1(a, 1)
+        for i in range(PACK, SLICES):
+            make_factor(i)
         round_q(0, q_raw[0])
         round_q(1, q_raw[1])
         gather_page(1, homes[2][:, 0:NP])
@@ -346,17 +361,17 @@ def tile_list_darts_slot_scores_kernel(
         make_x(1, x_rows[0][:, 1, :])
         make_x(2, x_rows[0][:, 2, :])
         gather_page(3, homes[2][:, 0:NP])
-        for i in range(PACK, SLICES):
-            first_products(i)
+        first_products(1)
         take_min(4)
         make_x(3, x_rows[0][:, 3, :])
         take_min(5)
         subtract_and_tanh(4)
         subtract_and_tanh(5)
         quantize_q(0)
-        for n in range(pieces):
-            interleave(page_bf[0][n], staged[n // 2][:, :, n % 2 * PIECE : (n % 2 + 1) * PIECE], 0)
-        house_x(0, staged[1][:, 0:2, :].rearrange("p t m -> p (t m)"))
+        for n in range(pieces - 1):
+            interleave(page_bf[0][n], staged[0][:, :, columns(n)], 0)
+        interleave(page_bf[0][pieces - 1], staged[1][:], 0)
+        house_x(0, staged[0][:, 0:2, :].rearrange("p t m -> p (t m)"))
         interleave(x_bf[0], x_rows[0][:], 0)
 
         staged_pair = raw_tile([P, 2, T2], "staged_pair")
@@ -372,12 +387,13 @@ def tile_list_darts_slot_scores_kernel(
         quantize_x(0)
         q_w[1] = kept([P, NP], U32, "q_w1", "x_rows0")
         quantize_q(1)
-        for n in range(pieces):
-            interleave(page_bf[1][n], staged_pair[:, :, n * PIECE : (n + 1) * PIECE], 0)
-        take_min(6, staged[1][:, 0, :])
-        take_min(7, staged[1][:, 1, :])
-        subtract_and_tanh(6)
+        for n in range(pieces - 1):
+            interleave(page_bf[1][n], staged_pair[:, :, columns(n)], 0)
+        take_min(6, staged[0][:, 0, :])
+        take_min(7, staged[0][:, 1, :])
+        subtract_and_tanh(6, page_home[1][pieces - 1][:, 0:S])
         subtract_and_tanh(7, homes[0][:, 0:S])
+        interleave(page_bf[1][pieces - 1], staged_pair[:, :, columns(pieces - 1)], 0)
         house_x(1, homes[0][:])
         interleave(x_bf[1], x_rows[1][:], 0)
 
@@ -391,10 +407,7 @@ def tile_list_darts_slot_scores_kernel(
             scatter(i)
             for n in range(pieces):
                 round_page_slice(i, n)
-        late_w = kept([P, 2 * PIECE], U32, "late_w", "wgs_t3")
-        for n in (2, 3):
-            page_w[0][n] = late_w[:, (n - 2) * PIECE : (n - 1) * PIECE]
-            quantize_page(0, n)
+        quantize_page(0, 2, "wgs_t3")
         for c in range(MT // 2, MT):
             open_f(c)
         gather_page(6)
@@ -405,7 +418,6 @@ def tile_list_darts_slot_scores_kernel(
         quantize_page(1, 2)
         make_x(7, x_bf[1][:, :, 3])
         quantize_x(1)
-        quantize_page(1, 3)
         for c in range(MT):
             second_pass(f_sum[c], c, 1, q_w, q_s)
             nc.scalar.copy(caps[c][:], f_sum[c][:])
@@ -421,9 +433,7 @@ def tile_list_darts_slot_scores_kernel(
                 cols = slice(part * NP // parts, (part + 1) * NP // parts)
                 result = caps[c][:, cols]
                 nc.vector.tensor_tensor(result, e_sum[c][:, cols], result, ALU.mult)
-                if c in (0, 1, 2, 4):
-                    nc.gpsimd.tensor_scalar(result, result, 1.0, slot_c, ALU.mult, ALU.add)
-                elif part == 0:
+                if c > 0 and part == 0:
                     nc.scalar.activation(result, result, ACT.Identity, bias=slot_c)
                 else:
                     nc.vector.tensor_scalar(result, result, slot_c, None, ALU.add)

import itertools
from contextlib import ExitStack

import concourse.mybir as mybir

K, H, T, S, T2, NP = 1536, 1024, 2048, 512, 1024, 512
FLOPS = 2 * (2 * K * H * S + 2 * H * T2 * NP)

F32 = mybir.dt.float32
BF16 = mybir.dt.bfloat16
I32 = mybir.dt.int32
U32 = mybir.dt.uint32
U16 = mybir.dt.uint16
U8 = mybir.dt.uint8
FP8X4 = mybir.dt.float8_e4m3fn_x4
FP4X4 = mybir.dt.float4_e2m1fn_x4
ALU = mybir.AluOpType
ACT = mybir.ActivationFunctionType

P = 128
PACK = 4
KP = P * PACK
KA = K // KP
HB = H // KP
SLICES = HB * PACK
MT = T2 // P
PIECES = ((0, 256), (256, 256), (512, 512))
RUN = 4


def tile_list_darts_slot_scores_kernel(
    tc, tab_words, tab_scales, offs, offs2, offs3, w1, w4_words, w4_scales, cap, gain, page0, wgs, lows, vec, q, slot, out
):
    nc = tc.nc
    with ExitStack() as ctx:
        keep = ctx.enter_context(tc.tile_pool(name="keep", bufs=1))
        ring = ctx.enter_context(tc.tile_pool(name="ring", bufs=1))
        psum = ctx.enter_context(tc.psum_pool(name="psum", bufs=1))

        def kept(shape, dtype, name, tag=None):
            return keep.tile(shape, dtype, name=name, tag=tag or name, align_bytes=64)

        def ringed(shape, dtype, name, tag, bufs):
            return ring.tile(shape, dtype, name=name, tag=tag, bufs=bufs, align_bytes=64)

        def raw_tile(shape, name):
            return ringed(shape, F32, name, "raw", 5)

        def bank(n, name):
            return psum.tile([P, 512], F32, name=name, tag="bank%d" % n)

        def quantize(codes, scales, values):
            nc.vector.quantize_mx(out=codes.bitcast(FP8X4), scales=scales, in_=values)

        idx = keep.tile([P, S // 16], U16, name="idx")
        idx2 = keep.tile([P, S // 16], U16, name="idx2")
        idx3 = keep.tile([P, NP // 16], U16, name="idx3")

        tab_s = kept([P, KA, T], U8, "tab_s")
        w4_s_raw = kept([P, KA, H], U8, "w4_s_raw")
        v_s = kept([P, KA, S], U8, "v_s")
        for engine, scales in ((nc.vector, tab_s), (nc.gpsimd, w4_s_raw), (nc.vector, v_s)):
            engine.memset(scales[:].rearrange("p a n -> p (a n)").bitcast(I32), 0)

        vectors = kept([P, HB, P], F32, "vectors")
        nc.vector.memset(vectors[:], 0.0)

        warm = kept([P, 2], F32, "warm")
        nc.vector.memset(warm[:, 0:1], 0.0)
        warm_out = kept([P, 1], F32, "warm_out")
        nc.scalar.activation(warm_out[:], warm[:, 0:1], ACT.Tanh)

        tab_w = [kept([P, T], I32, "tab_w%d" % a) for a in range(KA)]

        def load_tab(a):
            nc.sync.dma_start(tab_w[a][:], tab_words[a].rearrange("p n i -> p (n i)").bitcast(I32))

        w1_rows = w1.rearrange("(a p j) c -> a p j c", p=P, j=PACK)

        def load_w1(a, c0, width):
            raw = raw_tile([P, PACK, width], "w1_raw%d_%d" % (a, c0))
            nc.sync.dma_start(raw[:], w1_rows[a][:, :, c0 : c0 + width])
            return raw

        cap_rows = cap.rearrange("(b u t e) s -> b t u e s", b=HB, t=PACK, e=RUN)
        page_rows = page0.rearrange("(b u t e) m -> b t u e m", b=HB, t=PACK, e=RUN)
        caps, pages = {}, {}

        def load_cap(i):
            caps[i] = kept([P, S], F32, "cap%d" % i)
            nc.sync.dma_start(caps[i][:], cap_rows[i // PACK][i % PACK])

        def load_page(i):
            pages[i] = kept([P, T2], F32, "page%d" % i)
            nc.sync.dma_start(pages[i][:], page_rows[i // PACK][i % PACK])

        nc.sync.dma_start(idx[:], offs)
        first_words = tab_words[0].rearrange("p n i -> p (n i)").bitcast(I32)

        def load_first_words(part):
            cols = slice(part * (T // 4), (part + 1) * (T // 4))
            nc.sync.dma_start(tab_w[0][:, cols], first_words[:, cols])

        for part in range(3):
            load_first_words(part)
        nc.sync.dma_start(idx2[:], offs2)
        nc.sync.dma_start(idx3[:], offs3)
        for raw_scales, scales in ((w4_s_raw, w4_scales), (tab_s, tab_scales)):
            nc.sync.dma_start(raw_scales[0:P:8].bitcast(I32), scales.rearrange("a g n -> g a n").bitcast(I32))
        load_first_words(3)
        w4_raw = kept([P, KA, H // 2], I32, "w4_raw")
        nc.sync.dma_start(w4_raw[:], w4_words.rearrange("a p n -> p a n").bitcast(I32))
        w1_raw = {}
        w1_raw[0, 0] = load_w1(0, 0, KP)
        load_tab(1)
        for row, vector in enumerate((gain, lows, vec)):
            nc.sync.dma_start(vectors[row:P:32], vector.rearrange("(b g c) -> g b c", b=HB, g=4))
        w1_raw[1, 0] = load_w1(1, 0, KP)
        w1_raw[2, 0] = load_w1(2, 0, KP)
        load_tab(2)
        for i in range(PACK):
            load_cap(i)
        wgs_rows = wgs.rearrange("(u t e) s -> t u e s", t=PACK, e=RUN)
        wgs_t = [kept([P, S], F32, "wgs_t%d" % t) for t in range(PACK)]

        def load_wgs(t):
            for quad in range(4):
                nc.sync.dma_start(wgs_t[t][32 * quad : 32 * quad + 32], wgs_rows[t])

        for t in range(2):
            load_wgs(t)
            load_page(t)
        w1_raw[0, 1] = load_w1(0, KP, KP)
        load_wgs(2)
        load_page(2)
        w1_raw[1, 1] = load_w1(1, KP, KP)
        load_wgs(3)
        w1_raw[2, 1] = load_w1(2, KP, KP)
        load_page(3)
        load_cap(4)
        load_cap(5)

        v_w = [kept([P, S], U32, "v_w%d" % a) for a in range(KA)]
        picked_s = kept([P, KA, S], U8, "picked_s")

        def gather_words(a):
            nc.vector.tensor_copy(v_w[a][:], tab_w[a][:].bitcast(U32).indirect(idx[:]))

        w4_s = kept([P, KA * HB, PACK, P], U8, "w4_s")
        nc.vector.tensor_copy(
            w4_s[:].bitcast(I32).rearrange("p g t u -> p g u t"),
            w4_s_raw[:].bitcast(I32).rearrange("p a (b u t) -> p (a b) u t", b=HB, t=PACK),
        )
        for r in range(1, 4):
            nc.gpsimd.dma_start(w4_s[r:P:32].bitcast(I32), w4_s[8 * r : P : 32].bitcast(I32))
        for a in range(KA):
            nc.vector.tensor_copy(picked_s[:, a, :], tab_s[:, a, :].indirect(idx[:]))
        for r in range(4):
            nc.gpsimd.dma_start(v_s[r:P:32].bitcast(I32), picked_s[8 * r : P : 32].bitcast(I32))
        gather_words(0)
        w4_w = kept([P, KA * HB, PACK, P // 2], I32, "w4_w")
        nc.vector.tensor_copy(
            w4_w[:].rearrange("p g t (u e) -> p g u t e", e=2),
            w4_raw[:].rearrange("p a (b u t e) -> p (a b) u t e", b=HB, t=PACK, e=2),
        )

        vectors_dealt = kept([P, SLICES * 32], F32, "vectors_dealt")
        nc.vector.tensor_copy(
            vectors_dealt[:].rearrange("p (b t u e) -> p b u t e", b=HB, t=PACK, e=RUN),
            vectors[:].rearrange("p b (u t e) -> p b u t e", t=PACK, e=RUN),
        )
        per_row = kept([P, SLICES * 32], F32, "per_row")
        nc.vector.transpose(per_row[:], vectors_dealt[:])

        w1_w, w1_s = {}, {}
        homes = [kept([P, KP * PACK // 2], F32, "home%d" % a) for a in range(KA)]

        def round_w1(a, b):
            nc.scalar.copy(
                homes[a][:].bitcast(BF16).rearrange("p (t u e j) -> p u t j e", t=PACK, e=RUN, j=PACK),
                w1_raw[a, b][:].rearrange("p j (u t e) -> p u t j e", t=PACK, e=RUN),
            )

        def quantize_w1(a, b):
            w1_w[a, b] = kept([P, KP], U32, "w1_w%d_%d" % (a, b))
            w1_s[a, b] = kept([P, KP], U8, "w1_s%d_%d" % (a, b))
            quantize(w1_w[a, b][:], w1_s[a, b][:], homes[a][:].bitcast(BF16))

        def round_w1_shared(a):
            raw_halves = w1_raw[a, 0][:].rearrange("p j (h u t e) -> p h u t j e", h=2, t=PACK, e=RUN)
            halves = homes[a][:].bitcast(BF16).rearrange("p (t h u e j) -> p h u t j e", t=PACK, h=2, e=RUN, j=PACK)
            nc.scalar.copy(halves[:, 0], raw_halves[:, 0])
            nc.vector.tensor_copy(halves[:, 1], raw_halves[:, 1])

        round_w1(0, 0)
        gather_words(1)
        quantize_w1(0, 0)
        for a in range(1, KA):
            round_w1_shared(a)
            quantize_w1(a, 0)
        gather_words(2)

        sums, lesser, factors, picked = {}, {}, {}, {}

        def first_products(b):
            for t in range(PACK):
                sums[b * PACK + t] = (bank(2 * t, "a_sum%d_%d" % (b, t)), bank(2 * t + 1, "b_sum%d_%d" % (b, t)))
            order = list(itertools.product(range(KA), range(2))) + [(a, t) for t in range(2, PACK) for a in range(KA)]
            for a, t in order:
                a_sum, b_sum = sums[b * PACK + t]
                cols = slice(t * P, (t + 1) * P)
                nc.tensor.matmul_mx(
                    out=a_sum[:],
                    lhsT=w1_w[a, b][:, cols].bitcast(FP8X4),
                    lhsT_scale=w1_s[a, b][:, cols],
                    rhs=v_w[a][:].bitcast(FP8X4),
                    rhs_scale=v_s[:, a, :],
                    start=(a == 0),
                    stop=(a == KA - 1),
                )
                nc.tensor.matmul_mx(
                    out=b_sum[:],
                    lhsT=w4_w[:, a * HB + b, t, :].bitcast(FP4X4),
                    lhsT_scale=w4_s[:, a * HB + b, t, :],
                    rhs=v_w[a][:].bitcast(FP8X4),
                    rhs_scale=v_s[:, a, :],
                    start=(a == 0),
                    stop=(a == KA - 1),
                )

        def take_min(i, home=None):
            lesser[i] = caps[i][:] if home is None else home
            nc.vector.tensor_tensor(lesser[i], sums[i][0][:], caps[i][:], ALU.min)

        def subtract_and_tanh(i, home=None):
            diff = caps[i][:] if home is None else home
            nc.vector.tensor_tensor(diff, sums[i][1][:], lesser[i], ALU.subtract)
            nc.scalar.activation(caps[i][:], diff, ACT.Tanh)

        for t in range(PACK):
            factors[t] = kept([P, S], F32, "factor%d" % t)
            factors[t + PACK] = wgs_t[t]

        def make_factor(i):
            nc.scalar.activation(factors[i][:], wgs_t[i % PACK][:], ACT.Copy, scale=per_row[:, 32 * i : 32 * i + 1])

        def scatter(i):
            nc.vector.tensor_tensor(pages[i][:].indirect(idx2[:]), caps[i][:], factors[i][:], ALU.mult)

        def gather_page(i, home=None):
            picked[i] = ringed([P, NP], F32, "picked%d" % i, "picked", 2)[:] if home is None else home
            nc.vector.tensor_copy(picked[i], pages[i][:].indirect(idx3[:]))

        def make_x(i, target):
            nc.vector.tensor_scalar(
                target, picked[i], per_row[:, 32 * i + 1 : 32 * i + 2], per_row[:, 32 * i + 2 : 32 * i + 3], ALU.max, ALU.mult
            )

        def interleave(target, rows, t0):
            n = rows.shape[1]
            nc.scalar.copy(
                target[:, :, t0 : t0 + n].rearrange("p (c i) t -> p c t i", i=4),
                rows.rearrange("p t (c i) -> p c t i", i=4),
            )

        x_rows = [kept([P, PACK, NP], BF16, "x_rows0"), kept([P, 2, NP], BF16, "x_rows1")]
        x_home, x_bf = {}, {}

        def house_x(b, home):
            x_home[b] = home
            x_bf[b] = home.bitcast(BF16).rearrange("p (n t) -> p n t", t=PACK)

        x_w = [kept([P, NP], U32, "x_w%d" % b) for b in range(HB)]
        x_s = [kept([P, NP], U8, "x_s%d" % b) for b in range(HB)]
        q_w = {0: kept([P, NP], U32, "q_w0")}
        q_s = [kept([P, NP], U8, "q_s%d" % b) for b in range(HB)]
        pieces = len(PIECES)
        page_home = [[kept([P, PIECES[n][1] * PACK // 2], F32, "page_bf%d_%d" % (b, n)) for n in range(pieces)] for b in range(HB)]
        page_bf = [[home[:].bitcast(BF16).rearrange("p (n t) -> p n t", t=PACK) for home in homes] for homes in page_home]
        page_w = {}
        page_s = [[kept([P, PIECES[n][1]], U8, "page_s%d_%d" % (b, n)) for n in range(pieces)] for b in range(HB)]

        def columns(n):
            return slice(PIECES[n][0], PIECES[n][0] + PIECES[n][1])

        def quantize_x(b):
            quantize(x_w[b][:], x_s[b][:], x_home[b].bitcast(BF16))

        def quantize_page(b, n, tag=None):
            page_w[b, n] = kept([P, PIECES[n][1]], U32, "page_w%d_%d" % (b, n), tag)
            quantize(page_w[b, n][:], page_s[b][n][:], page_home[b][n][:].bitcast(BF16))

        def round_q(b, raw):
            interleave(homes[b][:].bitcast(BF16).rearrange("p (n t) -> p n t", t=PACK), raw[:], 0)

        def quantize_q(b):
            quantize(q_w[b][:], q_s[b][:], homes[b][:].bitcast(BF16))

        def round_page_slice(i, n):
            b, t = divmod(i, PACK)
            nc.scalar.copy(page_bf[b][n][:, :, t], pages[i][:, columns(n)])

        q_rows = q.rearrange("(b u t e) s -> b t u e s", b=HB, t=PACK, e=RUN)
        e_sum, f_sum = {}, {}

        def second_pass(acc, c, b, moving_w, moving_s):
            n = min(c // 2, pieces - 1)
            cols = slice(c * P - PIECES[n][0], (c + 1) * P - PIECES[n][0])
            nc.tensor.matmul_mx(
                out=acc[:],
                lhsT=page_w[b, n][:, cols].bitcast(FP8X4),
                lhsT_scale=page_s[b][n][:, cols],
                rhs=moving_w[b][:].bitcast(FP8X4),
                rhs_scale=moving_s[b][:],
                start=(b == 0),
                stop=(b == HB - 1),
            )

        def load_q(b):
            raw = raw_tile([P, PACK, NP], "q_raw%d" % b)
            for t in range(PACK):
                nc.sync.dma_start(raw[:, t, :], q_rows[b][t])
            return raw

        q_raw = [load_q(b) for b in range(HB)]
        load_page(4)
        load_page(5)

        first_products(0)
        for i in range(PACK):
            take_min(i, factors[i][:])
            subtract_and_tanh(i)
            make_factor(i)
        scatter(0)
        scatter(1)
        gather_page(0)
        scatter(2)
        make_x(0, x_rows[0][:, 0, :])
        scatter(3)
        staged = [raw_tile([P, PACK, T2 // 2], "staged%d" % half) for half in range(2)]
        for half in range(2):
            for t in range(PACK):
                nc.sync.dma_start(staged[half][:, t, :], pages[t][:, half * (T2 // 2) : (half + 1) * (T2 // 2)])
        load_cap(6)
        load_cap(7)
        load_page(6)
        load_page(7)
        slot_t = kept([P, MT], F32, "slot_t")
        with nc.allow_non_contiguous_dma(reason="one value of slot for each output row"):
            nc.sync.dma_start(slot_t[:], slot.rearrange("(c p) -> p c", p=P))

        for a in range(KA):
            round_w1(a, 1)
            quantize_w1(a, 1)
        for i in range(PACK, SLICES):
            make_factor(i)
        round_q(0, q_raw[0])
        round_q(1, q_raw[1])
        gather_page(1, homes[2][:, 0:NP])
        gather_page(2, homes[2][:, NP : 2 * NP])
        make_x(1, x_rows[0][:, 1, :])
        make_x(2, x_rows[0][:, 2, :])
        gather_page(3, homes[2][:, 0:NP])
        first_products(1)
        take_min(4)
        make_x(3, x_rows[0][:, 3, :])
        take_min(5)
        subtract_and_tanh(4)
        subtract_and_tanh(5)
        quantize_q(0)
        for n in range(pieces - 1):
            interleave(page_bf[0][n], staged[0][:, :, columns(n)], 0)
        interleave(page_bf[0][pieces - 1], staged[1][:], 0)
        house_x(0, staged[0][:, 0:2, :].rearrange("p t m -> p (t m)"))
        interleave(x_bf[0], x_rows[0][:], 0)

        staged_pair = raw_tile([P, 2, T2], "staged_pair")
        for t in range(2):
            scatter(PACK + t)
            nc.sync.dma_start(staged_pair[:, t, :], pages[PACK + t][:])
        gather_page(4)
        quantize_page(0, 0)
        quantize_page(0, 1)
        gather_page(5)
        make_x(4, x_rows[1][:, 0, :])
        make_x(5, x_rows[1][:, 1, :])
        quantize_x(0)
        q_w[1] = kept([P, NP], U32, "q_w1", "x_rows0")
        quantize_q(1)
        for n in range(pieces - 1):
            interleave(page_bf[1][n], staged_pair[:, :, columns(n)], 0)
        take_min(6, staged[0][:, 0, :])
        take_min(7, staged[0][:, 1, :])
        subtract_and_tanh(6, page_home[1][pieces - 1][:, 0:S])
        subtract_and_tanh(7, homes[0][:, 0:S])
        interleave(page_bf[1][pieces - 1], staged_pair[:, :, columns(pieces - 1)], 0)
        house_x(1, homes[0][:])
        interleave(x_bf[1], x_rows[1][:], 0)

        def open_f(c):
            f_sum[c] = bank(c, "f_sum%d" % c)
            second_pass(f_sum[c], c, 0, q_w, q_s)

        for c in range(MT // 2):
            open_f(c)
        for i in (6, 7):
            scatter(i)
            for n in range(pieces):
                round_page_slice(i, n)
        quantize_page(0, 2, "wgs_t3")
        for c in range(MT // 2, MT):
            open_f(c)
        gather_page(6)
        make_x(6, x_bf[1][:, :, 2])
        quantize_page(1, 0)
        quantize_page(1, 1)
        gather_page(7, page_home[1][0][:])
        quantize_page(1, 2)
        make_x(7, x_bf[1][:, :, 3])
        quantize_x(1)
        for c in range(MT):
            second_pass(f_sum[c], c, 1, q_w, q_s)
            nc.scalar.copy(caps[c][:], f_sum[c][:])
        for c in range(MT):
            e_sum[c] = bank(c, "e_sum%d" % c)
            for b in range(HB):
                second_pass(e_sum[c], c, b, x_w, x_s)

        for c in range(MT):
            slot_c = slot_t[:, c : c + 1]
            parts = 1 if c < MT - 1 else 2
            for part in range(parts):
                cols = slice(part * NP // parts, (part + 1) * NP // parts)
                result = caps[c][:, cols]
                nc.vector.tensor_tensor(result, e_sum[c][:, cols], result, ALU.mult)
                if c > 0 and part == 0:
                    nc.scalar.activation(result, result, ACT.Identity, bias=slot_c)
                else:
                    nc.vector.tensor_scalar(result, result, slot_c, None, ALU.add)
                nc.sync.dma_start(out[c * P : (c + 1) * P, cols], result)
